import numpy as np
import ml_dtypes

BF16 = ml_dtypes.bfloat16


def bf(x):
    return np.asarray(x, np.float32).astype(BF16)


def f32(x):
    return np.asarray(x, np.float32)


def f64(x):
    return np.asarray(x).astype(np.float64)


def striped(idx):
    return np.concatenate([l.reshape(-1, 16).T for l in idx])


def rows(idx, k):
    return np.tile(np.repeat(idx, 16, axis=0), (k // (16 * 8), 1))


def look(tab, idx):
    return np.take_along_axis(f64(tab), rows(idx, len(tab)), axis=1)


K, S, D, V, N, M = 128, 2048, 2, 1024, 2048, 128


def setup_inputs():
    return {"tab": f32(np.random.standard_normal((K, S))), "x0": f32(1.0 * np.random.standard_normal((K, V))), "w": bf(np.random.standard_normal((K, M)) / np.sqrt(K)), "b": f32(0.5 * np.random.standard_normal((M, 1))), "offs": striped(np.stack([np.random.permutation(S)[:N] for _ in range(8)]))}


def reference(tab, x0, w, b, offs):
    idx = np.stack([g.T.reshape(-1) for g in np.split(offs, 8)])
    m = f64(x0)
    for d in range(D):
        m = np.maximum(m, look(tab, idx[:, d * V:(d + 1) * V]))
    x = m + np.log(np.exp(f64(x0) - m) + sum(np.exp(look(tab, idx[:, d * V:(d + 1) * V]) - m) for d in range(D)))
    return np.maximum(f64(w).T @ x + f64(b), 0.0)

@@ -1,0 +1,73 @@
+import concourse.mybir as mybir
+
+F32, BF16, U16 = mybir.dt.float32, mybir.dt.bfloat16, mybir.dt.uint16
+ALU = mybir.AluOpType
+ACT = mybir.ActivationFunctionType
+
+P = 128
+V = 1024
+S = 2048
+N = 2 * V
+C = 512
+PER = 16
+
+FLOPS = 2 * P * P * V
+
+
+def tile_lookup_lse_relu_kernel(tc, tab, x0, w, b, offs, out):
+    nc = tc.nc
+    with (
+        tc.tile_pool(name="held", bufs=1) as held,
+        tc.tile_pool(name="work", bufs=2) as work,
+        tc.psum_pool(name="psum", bufs=2) as psum,
+    ):
+        offsets = held.tile([P, N // PER], U16, name="offsets")
+        table = held.tile([P, S], F32, name="table")
+        node = held.tile([P, V], F32, name="node")
+        weights = held.tile([P, P], BF16, name="weights")
+        bias = held.tile([P, 1], F32, name="bias")
+        nc.sync.dma_start(offsets[:], offs)
+        nc.sync.dma_start(table[:], tab)
+        for c in range(V // C):
+            nc.sync.dma_start(node[:, c * C : (c + 1) * C], x0[:, c * C : (c + 1) * C])
+        nc.scalar.dma_start(weights[:], w)
+        nc.scalar.dma_start(bias[:], b)
+
+        for c in range(V // C):
+            cols = slice(c * C, (c + 1) * C)
+            list0 = offsets[:, c * C // PER : (c + 1) * C // PER]
+            list1 = offsets[:, (V + c * C) // PER : (V + (c + 1) * C) // PER]
+
+            m0 = work.tile([P, C], F32, name="m0")
+            h = work.tile([P, C], F32, name="h")
+            nc.vector.tensor_tensor(m0[:], table[:].indirect(list0), node[:, cols], ALU.max)
+            nc.vector.tensor_tensor(h[:], table[:].indirect(list1), m0[:], ALU.max)
+
+            d0 = work.tile([P, C], F32, name="d0")
+            d1 = work.tile([P, C], F32, name="d1")
+            dx = work.tile([P, C], F32, name="dx")
+            nc.vector.tensor_tensor(dx[:], node[:, cols], h[:], ALU.subtract)
+            nc.vector.tensor_tensor(d0[:], table[:].indirect(list0), h[:], ALU.subtract)
+            nc.vector.tensor_tensor(d1[:], table[:].indirect(list1), h[:], ALU.subtract)
+
+            e0 = work.tile([P, C], F32, name="e0")
+            e1 = work.tile([P, C], F32, name="e1")
+            ex = work.tile([P, C], F32, name="ex")
+            nc.scalar.activation(ex[:], dx[:], ACT.Exp)
+            nc.scalar.activation(e0[:], d0[:], ACT.Exp)
+            nc.scalar.activation(e1[:], d1[:], ACT.Exp)
+
+            s0 = work.tile([P, C], F32, name="s0")
+            s1 = work.tile([P, C], F32, name="s1")
+            nc.vector.tensor_tensor(s0[:], ex[:], e0[:], ALU.add)
+            nc.vector.tensor_tensor(s1[:], s0[:], e1[:], ALU.add)
+            log_s = work.tile([P, C], F32, name="log_s")
+            nc.scalar.activation(log_s[:], s1[:], ACT.Ln)
+            x = work.tile([P, C], BF16, name="x")
+            nc.vector.tensor_tensor(x[:], h[:], log_s[:], ALU.add)
+
+            product = psum.tile([P, C], F32, name="product")
+            nc.tensor.matmul(product[:], weights[:], x[:], start=True, stop=True)
+            result = work.tile([P, C], F32, name="result")
+            nc.scalar.activation(result[:], product[:], ACT.Relu, bias=bias[:, 0:1])
+            nc.sync.dma_start(out[:, cols], result[:])

@@ -9,17 +9,24 @@ V = 1024
 S = 2048
 N = 2 * V
 C = 512
+CHUNKS = V // C
+H = 256
 PER = 16
 
 FLOPS = 2 * P * P * V
+
+
+def entries(offsets, d, c):
+    first = (d * V + c * C) // PER
+    return offsets[:, first : first + C // PER]
 
 
 def tile_lookup_lse_relu_kernel(tc, tab, x0, w, b, offs, out):
     nc = tc.nc
     with (
         tc.tile_pool(name="held", bufs=1) as held,
-        tc.tile_pool(name="work", bufs=2) as work,
-        tc.psum_pool(name="psum", bufs=2) as psum,
+        tc.psum_pool(name="psum", bufs=1) as psum,
+        tc.psum_pool(name="products", bufs=4) as products,
     ):
         offsets = held.tile([P, N // PER], U16, name="offsets")
         table = held.tile([P, S], F32, name="table")
@@ -28,46 +35,50 @@ def tile_lookup_lse_relu_kernel(tc, tab, x0, w, b, offs, out):
         bias = held.tile([P, 1], F32, name="bias")
         nc.sync.dma_start(offsets[:], offs)
         nc.sync.dma_start(table[:], tab)
-        for c in range(V // C):
+        for c in range(CHUNKS):
             nc.sync.dma_start(node[:, c * C : (c + 1) * C], x0[:, c * C : (c + 1) * C])
         nc.scalar.dma_start(weights[:], w)
         nc.scalar.dma_start(bias[:], b)
 
-        for c in range(V // C):
-            cols = slice(c * C, (c + 1) * C)
-            list0 = offsets[:, c * C // PER : (c + 1) * C // PER]
-            list1 = offsets[:, (V + c * C) // PER : (V + (c + 1) * C) // PER]
+        m0 = held.tile([P, V], F32, name="m0")
+        h = held.tile([P, V], F32, name="h")
+        d0 = held.tile([P, V], F32, name="d0")
+        d1 = held.tile([P, V], F32, name="d1")
+        e0 = held.tile([P, V], F32, name="e0")
+        e1 = held.tile([P, V], F32, name="e1")
+        ex = held.tile([P, V], F32, name="ex")
+        s0 = held.tile([P, V], F32, name="s0")
+        s1 = held.tile([P, V], F32, name="s1")
+        log_s = held.tile([P, V], F32, name="log_s")
+        x = held.tile([P, V], BF16, name="x")
+        result = held.tile([P, V], F32, name="result")
+        dx = held.tile([P, V], F32, name="dx")
+        chunks = [slice(c * C, (c + 1) * C) for c in range(CHUNKS)]
 
-            m0 = work.tile([P, C], F32, name="m0")
-            h = work.tile([P, C], F32, name="h")
-            nc.vector.tensor_tensor(m0[:], table[:].indirect(list0), node[:, cols], ALU.max)
-            nc.vector.tensor_tensor(h[:], table[:].indirect(list1), m0[:], ALU.max)
+        for c, cols in enumerate(chunks):
+            nc.vector.tensor_tensor(m0[:, cols], table[:].indirect(entries(offsets, 0, c)), node[:, cols], ALU.max)
+        for c, cols in enumerate(chunks):
+            nc.vector.tensor_tensor(h[:, cols], table[:].indirect(entries(offsets, 1, c)), m0[:, cols], ALU.max)
 
-            d0 = work.tile([P, C], F32, name="d0")
-            d1 = work.tile([P, C], F32, name="d1")
-            dx = work.tile([P, C], F32, name="dx")
-            nc.vector.tensor_tensor(dx[:], node[:, cols], h[:], ALU.subtract)
-            nc.vector.tensor_tensor(d0[:], table[:].indirect(list0), h[:], ALU.subtract)
-            nc.vector.tensor_tensor(d1[:], table[:].indirect(list1), h[:], ALU.subtract)
+        for c, cols in enumerate(chunks):
+            nc.vector.tensor_tensor(dx[:, cols], node[:, cols], h[:, cols], ALU.subtract)
+            nc.vector.tensor_tensor(d0[:, cols], table[:].indirect(entries(offsets, 0, c)), h[:, cols], ALU.subtract)
+            nc.vector.tensor_tensor(d1[:, cols], table[:].indirect(entries(offsets, 1, c)), h[:, cols], ALU.subtract)
+            nc.scalar.activation(ex[:, cols], dx[:, cols], ACT.Exp)
+            nc.scalar.activation(e0[:, cols], d0[:, cols], ACT.Exp)
+            nc.scalar.activation(e1[:, cols], d1[:, cols], ACT.Exp)
 
-            e0 = work.tile([P, C], F32, name="e0")
-            e1 = work.tile([P, C], F32, name="e1")
-            ex = work.tile([P, C], F32, name="ex")
-            nc.scalar.activation(ex[:], dx[:], ACT.Exp)
-            nc.scalar.activation(e0[:], d0[:], ACT.Exp)
-            nc.scalar.activation(e1[:], d1[:], ACT.Exp)
-
-            s0 = work.tile([P, C], F32, name="s0")
-            s1 = work.tile([P, C], F32, name="s1")
-            nc.vector.tensor_tensor(s0[:], ex[:], e0[:], ALU.add)
-            nc.vector.tensor_tensor(s1[:], s0[:], e1[:], ALU.add)
-            log_s = work.tile([P, C], F32, name="log_s")
-            nc.scalar.activation(log_s[:], s1[:], ACT.Ln)
-            x = work.tile([P, C], BF16, name="x")
-            nc.vector.tensor_tensor(x[:], h[:], log_s[:], ALU.add)
-
-            product = psum.tile([P, C], F32, name="product")
-            nc.tensor.matmul(product[:], weights[:], x[:], start=True, stop=True)
-            result = work.tile([P, C], F32, name="result")
-            nc.scalar.activation(result[:], product[:], ACT.Relu, bias=bias[:, 0:1])
-            nc.sync.dma_start(out[:, cols], result[:])
+        for cols in chunks:
+            nc.vector.tensor_tensor(s0[:, cols], ex[:, cols], e0[:, cols], ALU.add)
+            nc.vector.tensor_tensor(s1[:, cols], s0[:, cols], e1[:, cols], ALU.add)
+        for i in range(V // H):
+            cols = slice(i * H, (i + 1) * H)
+            nc.scalar.activation(log_s[:, cols], s1[:, cols], ACT.Ln)
+            nc.vector.tensor_tensor(x[:, cols], h[:, cols], log_s[:, cols], ALU.add)
+            product = products.tile([P, H], F32, name="product")
+            nc.tensor.matmul(product[:], weights[:], x[:, cols], start=True, stop=True)
+            if i % 2 == 0:
+                nc.scalar.activation(result[:, cols], product[:], ACT.Relu, bias=bias[:, 0:1])
+            else:
+                nc.vector.tensor_scalar(result[:, cols], product[:], bias[:, 0:1], 0.0, ALU.add, ALU.max)
+            nc.sync.dma_start(out[:, cols], result[:, cols])

@@ -37,8 +37,8 @@ def tile_lookup_lse_relu_kernel(tc, tab, x0, w, b, offs, out):
         nc.sync.dma_start(table[:], tab)
         for c in range(CHUNKS):
             nc.sync.dma_start(node[:, c * C : (c + 1) * C], x0[:, c * C : (c + 1) * C])
-        nc.scalar.dma_start(weights[:], w)
-        nc.scalar.dma_start(bias[:], b)
+        nc.sync.dma_start(weights[:], w)
+        nc.sync.dma_start(bias[:], b)
 
         m0 = held.tile([P, V], F32, name="m0")
         h = held.tile([P, V], F32, name="h")

@@ -1,4 +1,5 @@
 import concourse.mybir as mybir
+from concourse.masks import make_identity
 
 F32, BF16, U16 = mybir.dt.float32, mybir.dt.bfloat16, mybir.dt.uint16
 ALU = mybir.AluOpType
@@ -40,6 +41,11 @@ def tile_lookup_lse_relu_kernel(tc, tab, x0, w, b, offs, out):
         nc.sync.dma_start(weights[:], w)
         nc.sync.dma_start(bias[:], b)
 
+        plus = held.tile([P, P], F32, name="plus")
+        minus = held.tile([P, P], F32, name="minus")
+        make_identity(nc, plus[:])
+        nc.gpsimd.tensor_scalar(minus[:], plus[:], -1.0, 0.0, ALU.mult, ALU.add)
+
         m0 = held.tile([P, V], F32, name="m0")
         h = held.tile([P, V], F32, name="h")
         d0 = held.tile([P, V], F32, name="d0")
@@ -52,7 +58,8 @@ def tile_lookup_lse_relu_kernel(tc, tab, x0, w, b, offs, out):
         log_s = held.tile([P, V], F32, name="log_s")
         x = held.tile([P, V], BF16, name="x")
         result = held.tile([P, V], F32, name="result")
-        dx = held.tile([P, V], F32, name="dx")
+        dx_first = psum.tile([P, C], F32, name="dx_first")
+        dx_last = held.tile([P, C], F32, name="dx_last")
         chunks = [slice(c * C, (c + 1) * C) for c in range(CHUNKS)]
 
         for c, cols in enumerate(chunks):
@@ -60,17 +67,22 @@ def tile_lookup_lse_relu_kernel(tc, tab, x0, w, b, offs, out):
         for c, cols in enumerate(chunks):
             nc.vector.tensor_tensor(h[:, cols], table[:].indirect(entries(offsets, 1, c)), m0[:, cols], ALU.max)
 
+        nc.tensor.matmul(dx_first[:], plus[:], node[:, chunks[0]], start=True, stop=False)
+        nc.tensor.matmul(dx_first[:], minus[:], h[:, chunks[0]], start=False, stop=True)
+        nc.scalar.activation(ex[:, chunks[0]], dx_first[:], ACT.Exp)
+        nc.vector.tensor_tensor(dx_last[:], node[:, chunks[1]], h[:, chunks[1]], ALU.subtract)
+        nc.scalar.activation(ex[:, chunks[1]], dx_last[:], ACT.Exp)
+
         for c, cols in enumerate(chunks):
-            nc.vector.tensor_tensor(dx[:, cols], node[:, cols], h[:, cols], ALU.subtract)
             nc.vector.tensor_tensor(d0[:, cols], table[:].indirect(entries(offsets, 0, c)), h[:, cols], ALU.subtract)
-            nc.vector.tensor_tensor(d1[:, cols], table[:].indirect(entries(offsets, 1, c)), h[:, cols], ALU.subtract)
-            nc.scalar.activation(ex[:, cols], dx[:, cols], ACT.Exp)
             nc.scalar.activation(e0[:, cols], d0[:, cols], ACT.Exp)
+        for c, cols in enumerate(chunks):
+            nc.vector.tensor_tensor(d1[:, cols], table[:].indirect(entries(offsets, 1, c)), h[:, cols], ALU.subtract)
             nc.scalar.activation(e1[:, cols], d1[:, cols], ACT.Exp)
 
         for cols in chunks:
             nc.vector.tensor_tensor(s0[:, cols], ex[:, cols], e0[:, cols], ALU.add)
-            nc.vector.tensor_tensor(s1[:, cols], s0[:, cols], e1[:, cols], ALU.add)
+        nc.vector.tensor_tensor(s1[:], s0[:], e1[:], ALU.add)
         for i in range(V // H):
             cols = slice(i * H, (i + 1) * H)
             nc.scalar.activation(log_s[:, cols], s1[:, cols], ACT.Ln)

import concourse.mybir as mybir
from concourse.masks import make_identity

F32, BF16, U16 = mybir.dt.float32, mybir.dt.bfloat16, mybir.dt.uint16
ALU = mybir.AluOpType
ACT = mybir.ActivationFunctionType

P = 128
V = 1024
S = 2048
N = 2 * V
C = 512
CHUNKS = V // C
H = 256
PER = 16

FLOPS = 2 * P * P * V


def entries(offsets, d, c):
    first = (d * V + c * C) // PER
    return offsets[:, first : first + C // PER]


def tile_lookup_lse_relu_kernel(tc, tab, x0, w, b, offs, out):
    nc = tc.nc
    with (
        tc.tile_pool(name="held", bufs=1) as held,
        tc.psum_pool(name="psum", bufs=1) as psum,
        tc.psum_pool(name="products", bufs=4) as products,
    ):
        offsets = held.tile([P, N // PER], U16, name="offsets")
        table = held.tile([P, S], F32, name="table")
        node = held.tile([P, V], F32, name="node")
        weights = held.tile([P, P], BF16, name="weights")
        bias = held.tile([P, 1], F32, name="bias")
        nc.sync.dma_start(offsets[:], offs)
        nc.sync.dma_start(table[:], tab)
        for c in range(CHUNKS):
            nc.sync.dma_start(node[:, c * C : (c + 1) * C], x0[:, c * C : (c + 1) * C])
        nc.sync.dma_start(weights[:], w)
        nc.sync.dma_start(bias[:], b)

        plus = held.tile([P, P], F32, name="plus")
        minus = held.tile([P, P], F32, name="minus")
        make_identity(nc, plus[:])
        nc.gpsimd.tensor_scalar(minus[:], plus[:], -1.0, 0.0, ALU.mult, ALU.add)

        m0 = held.tile([P, V], F32, name="m0")
        h = held.tile([P, V], F32, name="h")
        d0 = held.tile([P, V], F32, name="d0")
        d1 = held.tile([P, V], F32, name="d1")
        e0 = held.tile([P, V], F32, name="e0")
        e1 = held.tile([P, V], F32, name="e1")
        ex = held.tile([P, V], F32, name="ex")
        s0 = held.tile([P, V], F32, name="s0")
        s1 = held.tile([P, V], F32, name="s1")
        log_s = held.tile([P, V], F32, name="log_s")
        x = held.tile([P, V], BF16, name="x")
        result = held.tile([P, V], F32, name="result")
        dx_first = psum.tile([P, C], F32, name="dx_first")
        dx_last = held.tile([P, C], F32, name="dx_last")
        chunks = [slice(c * C, (c + 1) * C) for c in range(CHUNKS)]

        for c, cols in enumerate(chunks):
            nc.vector.tensor_tensor(m0[:, cols], table[:].indirect(entries(offsets, 0, c)), node[:, cols], ALU.max)
        for c, cols in enumerate(chunks):
            nc.vector.tensor_tensor(h[:, cols], table[:].indirect(entries(offsets, 1, c)), m0[:, cols], ALU.max)

        nc.tensor.matmul(dx_first[:], plus[:], node[:, chunks[0]], start=True, stop=False)
        nc.tensor.matmul(dx_first[:], minus[:], h[:, chunks[0]], start=False, stop=True)
        nc.scalar.activation(ex[:, chunks[0]], dx_first[:], ACT.Exp)
        nc.vector.tensor_tensor(dx_last[:], node[:, chunks[1]], h[:, chunks[1]], ALU.subtract)
        nc.scalar.activation(ex[:, chunks[1]], dx_last[:], ACT.Exp)

        for c, cols in enumerate(chunks):
            nc.vector.tensor_tensor(d0[:, cols], table[:].indirect(entries(offsets, 0, c)), h[:, cols], ALU.subtract)
            nc.scalar.activation(e0[:, cols], d0[:, cols], ACT.Exp)
        for c, cols in enumerate(chunks):
            nc.vector.tensor_tensor(d1[:, cols], table[:].indirect(entries(offsets, 1, c)), h[:, cols], ALU.subtract)
            nc.scalar.activation(e1[:, cols], d1[:, cols], ACT.Exp)

        for cols in chunks:
            nc.vector.tensor_tensor(s0[:, cols], ex[:, cols], e0[:, cols], ALU.add)
        nc.vector.tensor_tensor(s1[:], s0[:], e1[:], ALU.add)
        for i in range(V // H):
            cols = slice(i * H, (i + 1) * H)
            nc.scalar.activation(log_s[:, cols], s1[:, cols], ACT.Ln)
            nc.vector.tensor_tensor(x[:, cols], h[:, cols], log_s[:, cols], ALU.add)
            product = products.tile([P, H], F32, name="product")
            nc.tensor.matmul(product[:], weights[:], x[:, cols], start=True, stop=True)
            if i % 2 == 0:
                nc.scalar.activation(result[:, cols], product[:], ACT.Relu, bias=bias[:, 0:1])
            else:
                nc.vector.tensor_scalar(result[:, cols], product[:], bias[:, 0:1], 0.0, ALU.add, ALU.max)
            nc.sync.dma_start(out[:, cols], result[:, cols])
